import numpy as np
import ml_dtypes


def mxq(x, axis, fmt="e4m3"):
    dtype, down = {"e4m3": (ml_dtypes.float8_e4m3fn, 7), "e5m2": (ml_dtypes.float8_e5m2, 14)}[fmt]
    v = np.moveaxis(np.asarray(x, np.float32).astype(ml_dtypes.bfloat16).astype(np.float64), axis, -1)
    blocks = v.reshape(v.shape[:-1] + (-1, 32))
    amax = np.abs(blocks).max(-1, keepdims=True)
    byte = np.maximum(np.where(amax > 0, np.frexp(amax)[1] - 1 + 127, 0) - down, 1)
    scale = np.exp2(byte - 127.0)
    codes = (blocks / scale).astype(np.float32).astype(dtype).astype(np.float64)
    return np.moveaxis((codes * scale).reshape(v.shape), -1, axis)


WIDE = False


def mx_kscale(k):
    if not WIDE:
        return np.ones(k)
    levels = np.array([10, -10, 5, -5, 0])
    if k % 512:
        return np.exp2(np.random.permutation(np.resize(levels, k // 32))).repeat(32)
    a = np.empty((k // 512, 16))
    for p in range(k // 512):
        a[p, :8] = np.random.permutation(np.resize(levels, 8))
        for g in range(8):
            far = levels[np.abs(levels - a[p, g]) >= 10]
            a[p, g + 8] = far[np.random.randint(len(far))]
    return np.exp2(a.ravel()).repeat(32)


def f64(x):
    return np.asarray(x).astype(np.float64)


def striped8(idx):
    return np.concatenate([x.reshape(-1, 16).T for x in idx]).astype(np.uint16)


def runs(offs, k):
    lists = np.stack([offs[16 * r : 16 * r + 16].T.reshape(-1) for r in range(8)]).astype(np.int64)
    return lists[np.arange(k) % 512 // 64]


def pack_weight(w):
    k, n = w.shape
    w = f64(np.asarray(w, np.float32).astype(ml_dtypes.bfloat16)).reshape(k // 32, 32, n)
    amax = np.abs(w).max(1)
    byte = np.clip(np.where(amax > 0, np.frexp(amax)[1] - 1 + 127 - 7, 1), 1, 254)
    scaled = (w * np.exp2(127.0 - byte)[:, None, :]).reshape(k, n).astype(np.float32)
    words = np.ascontiguousarray(scaled.reshape(k // 512, 128, 4, n).transpose(0, 1, 3, 2)).astype(ml_dtypes.float8_e4m3fn).view(np.uint8)
    return words, np.ascontiguousarray(byte.astype(np.uint8).reshape(k // 512, 16, n))


def unpack_weight(words, scales):
    g, p, n, _ = words.shape
    vals = np.ascontiguousarray(words).view(ml_dtypes.float8_e4m3fn).astype(np.float64) * np.repeat(np.exp2(scales.astype(np.float64) - 127.0), 8, axis=1)[..., None]
    return vals.transpose(0, 1, 3, 2).reshape(g * 512, n)


K, T, S, N, H = 512, 2048, 512, 512, 512


def setup_inputs():
    n = np.random.standard_normal
    s = mx_kscale(K)[:, None]
    u = mx_kscale(S)
    packed_xT = pack_weight(n((K, T)) * s)
    return {
        "x_words": packed_xT[0],
        "x_scales": packed_xT[1],
        "wa": (n((K, H)) / np.sqrt(K) / s).astype(np.float32),
        "wb": (n((K, N)) / np.sqrt(K) / s).astype(np.float32),
        "gt": (np.random.uniform(0.5, 1.5, (S, 1)) * u[:, None]).astype(np.float32),
        "gi": (np.random.uniform(0.5, 1.5, (S, 1)) / u[:, None]).astype(np.float32),
        "offs": striped8(np.stack([np.random.permutation(T)[:S] for _ in range(8)])),
    }


def reference(x_words, x_scales, wa, wb, gt, gi, offs):
    xq = unpack_weight(x_words, x_scales)[np.arange(K)[:, None], runs(offs, K)]
    a = xq.T @ mxq(f64(wa), 0, "e4m3")
    z = f64(gt) * np.exp(0.5 * a)
    b = xq.T @ mxq(f64(wb), 0, "e4m3")
    z2 = f64(gi) * b
    return 0.03125 * ((mxq(z, 0, "e4m3").T @ mxq(z2, 0, "e4m3")))

@@ -1,0 +1,207 @@
+from contextlib import ExitStack
+
+import concourse.mybir as mybir
+
+K, T, S, H, N = 512, 2048, 512, 512, 512
+FLOPS = 2 * K * S * H + 2 * K * S * N + 2 * S * H * N
+
+F32 = mybir.dt.float32
+BF16 = mybir.dt.bfloat16
+I32 = mybir.dt.int32
+U32 = mybir.dt.uint32
+U16 = mybir.dt.uint16
+U8 = mybir.dt.uint8
+FP8X4 = mybir.dt.float8_e4m3fn_x4
+ACT = mybir.ActivationFunctionType
+MULT = mybir.AluOpType.mult
+
+P = 128
+PACK = 4
+COLS = 128
+HALF = 256
+
+
+def tile_picked_expool_exp_p_kernel(tc, x_words, x_scales, wa, wb, gt, gi, offs, out):
+    nc = tc.nc
+    with ExitStack() as ctx:
+        keep = ctx.enter_context(tc.tile_pool(name="keep", bufs=1))
+        psum = ctx.enter_context(tc.psum_pool(name="psum", bufs=1))
+
+        offsets = keep.tile([P, S // 16], U16, name="offsets")
+        nc.sync.dma_start(offsets[:], offs)
+
+        scale_table = keep.tile([P, T], U8, name="scale_table", align_bytes=64)
+        nc.vector.memset(scale_table[:].bitcast(I32), 0)
+        nc.sync.dma_start(scale_table[0:P:8, :].bitcast(I32), x_scales[0].bitcast(I32))
+        x_plane = keep.tile([P, S], U8, name="x_plane", align_bytes=64)
+        nc.vector.memset(x_plane[:].bitcast(I32), 0)
+
+        word_table = keep.tile([P, T], I32, name="word_table", align_bytes=64)
+        nc.sync.dma_start(word_table[:], x_words[0].rearrange("p c r -> p (c r)").bitcast(I32))
+
+        def load_half(w, half, name):
+            raw = keep.tile([P, PACK, HALF], F32, name=name, align_bytes=64)
+            nc.sync.dma_start(raw[:], w.rearrange("(p j) c -> p j c", j=PACK)[:, :, half * HALF : (half + 1) * HALF])
+            return raw
+
+        wb_raw = [load_half(wb, u, "wb_raw%d" % u) for u in range(2)]
+        wa_raw = [load_half(wa, u, "wa_raw%d" % u) for u in range(2)]
+
+        gi_sb = keep.tile([P, PACK], F32, name="gi_sb", align_bytes=64)
+        nc.gpsimd.dma_start(gi_sb[:], gi.rearrange("(p t) o -> p (t o)", t=PACK))
+        gt_sb = keep.tile([P, PACK], F32, name="gt_sb", align_bytes=64)
+        nc.gpsimd.dma_start(gt_sb[:], gt.rearrange("(p t) o -> p (t o)", t=PACK))
+
+        warm_in = keep.tile([P, 1], F32, name="warm_in")
+        warm_out = keep.tile([P, 1], F32, name="warm_out")
+        nc.gpsimd.memset(warm_in[:], 0.0)
+        nc.scalar.activation(warm_out[:], warm_in[:], ACT.Exp, scale=0.5)
+
+        picked_scales = keep.tile([P, S], U8, name="picked_scales", align_bytes=64)
+        nc.vector.tensor_copy(picked_scales[:], scale_table[:].indirect(offsets[:]))
+        dealt_scales = keep.tile([P, S], U8, name="dealt_scales", align_bytes=64)
+        nc.vector.tensor_copy(
+            dealt_scales[:].rearrange("p (t c i) -> p c t i", t=PACK, i=16),
+            picked_scales[:].rearrange("p (c i t) -> p c t i", t=PACK, i=16),
+        )
+        for q in range(4):
+            nc.scalar.dma_start(
+                x_plane[32 * q : 32 * q + 4, :].bitcast(I32),
+                dealt_scales[32 * q : 32 * q + 32 : 8, :].bitcast(I32),
+            )
+
+        picked_words = keep.tile([P, S], I32, name="picked_words", tag="picked_then_codes", align_bytes=64)
+        nc.vector.tensor_copy(picked_words[:].bitcast(U32), word_table[:].bitcast(U32).indirect(offsets[:]))
+        x_codes = keep.tile([P, S], I32, name="x_codes", align_bytes=64)
+        nc.vector.tensor_copy(
+            x_codes[:].rearrange("p (t c i) -> p c t i", t=PACK, i=4),
+            picked_words[:].rearrange("p (c i t) -> p c t i", t=PACK, i=4),
+        )
+
+        def tiles(name, count, width, dtype):
+            return [keep.tile([P, width], dtype, name="%s%d" % (name, n), align_bytes=64) for n in range(count)]
+
+        wb_bf = tiles("wb_bf", 2, PACK * HALF, BF16)
+        wa_bf = tiles("wa_bf", 2, PACK * HALF, BF16)
+        wb_codes = [
+            keep.tile([P, HALF], I32, name="wb_codes0", tag="picked_then_codes", align_bytes=64),
+            keep.tile([P, HALF], I32, name="wb_codes1", align_bytes=64),
+        ]
+        wb_plane = tiles("wb_plane", 2, HALF, U8)
+        wa_codes, wa_plane = tiles("wa_codes", 2, HALF, I32), tiles("wa_plane", 2, HALF, U8)
+        z2_bf = tiles("z2_bf", 2, PACK * HALF, BF16)
+        z_bf = tiles("z_bf", 4, PACK * COLS, BF16)
+        e_sb = tiles("e_sb", 4, PACK * COLS, F32)
+        z2_codes = keep.tile([P, N], I32, name="z2_codes", align_bytes=64)
+        z2_plane = keep.tile([P, N], U8, name="z2_plane", align_bytes=64)
+        z_codes, z_plane = tiles("z_codes", 4, COLS, I32), tiles("z_plane", 4, COLS, U8)
+        result = tiles("result", 4, N, F32)
+
+        def cast(copy, raw, bf, n):
+            u, v = divmod(n, 2)
+            copy(
+                bf[u][:, v * PACK * COLS : (v + 1) * PACK * COLS].rearrange("p (c i j) -> p c j i", i=4, j=PACK),
+                raw[u][:, :, v * COLS : (v + 1) * COLS].rearrange("p j (c i) -> p c j i", i=4),
+            )
+
+        def quantize(codes, plane, values):
+            nc.vector.quantize_mx(out=codes.bitcast(FP8X4), scales=plane, in_=values)
+
+        def project(codes, plane, n, bank):
+            u, v = divmod(n, 2)
+            acc = psum.tile([P, PACK, COLS], F32, name="acc", tag="bank%d" % bank)
+            cols = slice(v * COLS, (v + 1) * COLS)
+            for t in range(PACK):
+                places = slice(t * P, (t + 1) * P)
+                nc.tensor.matmul_mx(
+                    out=acc[:, t, :],
+                    lhsT=x_codes[:, places].bitcast(FP8X4),
+                    lhsT_scale=x_plane[:, places],
+                    rhs=codes[u][:, cols].bitcast(FP8X4),
+                    rhs_scale=plane[u][:, cols],
+                    start=True,
+                    stop=True,
+                )
+            return acc[:].rearrange("p t c -> p c t")
+
+        def weigh(dst, src, g):
+            nc.vector.tensor_tensor(
+                dst.rearrange("p (c t) -> p c t", t=PACK), src, g[:].unsqueeze(1).to_broadcast([P, COLS, PACK]), MULT
+            )
+
+        def values(n):
+            u, v = divmod(n, 2)
+            weigh(z2_bf[u][:, v * PACK * COLS : (v + 1) * PACK * COLS], project(wb_codes, wb_plane, n, n), gi_sb)
+
+        def quantize_values(u):
+            cols = slice(u * HALF, (u + 1) * HALF)
+            quantize(z2_codes[:, cols], z2_plane[:, cols], z2_bf[u][:])
+
+        def scores(n):
+            e = e_sb[n][:].rearrange("p (c t) -> p c t", t=PACK)
+            nc.scalar.activation(e, project(wa_codes, wa_plane, n, 4 + n), ACT.Exp, scale=0.5)
+
+        def weights(n):
+            weigh(z_bf[n][:], e_sb[n][:].rearrange("p (c t) -> p c t", t=PACK), gt_sb)
+
+        def quantize_weights(n):
+            quantize(z_codes[n][:], z_plane[n][:], z_bf[n][:])
+
+        def pool_part(n, cols, bank, on_vector):
+            acc = psum.tile([P, cols.stop - cols.start], F32, name="acc", tag="bank%d" % bank)
+            nc.tensor.matmul_mx(
+                out=acc[:],
+                lhsT=z_codes[n][:].bitcast(FP8X4),
+                lhsT_scale=z_plane[n][:],
+                rhs=z2_codes[:, cols].bitcast(FP8X4),
+                rhs_scale=z2_plane[:, cols],
+                start=True,
+                stop=True,
+            )
+            if on_vector:
+                nc.vector.tensor_scalar_mul(result[n][:, cols], acc[:], 0.03125)
+            else:
+                nc.scalar.activation(result[n][:, cols], acc[:], ACT.Copy, scale=0.03125)
+
+        def store(n):
+            nc.sync.dma_start(out[n * P : (n + 1) * P, :], result[n][:])
+
+        def pool_out(n):
+            quantize_weights(n)
+            pool_part(n, slice(0, N), n, False)
+            store(n)
+
+        for v in range(2):
+            cast(nc.scalar.copy, wb_raw, wb_bf, v)
+            cols = slice(v * COLS, (v + 1) * COLS)
+            quantize(wb_codes[0][:, cols], wb_plane[0][:, cols], wb_bf[0][:, v * PACK * COLS : (v + 1) * PACK * COLS])
+        cast(nc.scalar.copy, wb_raw, wb_bf, 2)
+        cast(nc.scalar.copy, wb_raw, wb_bf, 3)
+        values(0)
+        values(1)
+        quantize(wb_codes[1][:], wb_plane[1][:], wb_bf[1][:])
+        cast(nc.scalar.copy, wa_raw, wa_bf, 0)
+        cast(nc.scalar.copy, wa_raw, wa_bf, 1)
+        quantize_values(0)
+        values(2)
+        quantize(wa_codes[0][:], wa_plane[0][:], wa_bf[0][:])
+        values(3)
+        cast(nc.scalar.copy, wa_raw, wa_bf, 2)
+        cast(nc.scalar.copy, wa_raw, wa_bf, 3)
+        quantize_values(1)
+        quantize(wa_codes[1][:], wa_plane[1][:], wa_bf[1][:])
+        scores(0)
+        scores(1)
+        weights(0)
+        scores(2)
+        weights(1)
+        scores(3)
+        pool_out(0)
+        weights(2)
+        pool_out(1)
+        pool_out(2)
+        weights(3)
+        quantize_weights(3)
+        pool_part(3, slice(0, HALF), 3, False)
+        pool_part(3, slice(HALF, N), 4, True)
+        store(3)

@@ -19,12 +19,14 @@ P = 128
 PACK = 4
 COLS = 128
 HALF = 256
+RAW_BYTES = PACK * HALF * 4
 
 
 def tile_picked_expool_exp_p_kernel(tc, x_words, x_scales, wa, wb, gt, gi, offs, out):
     nc = tc.nc
     with ExitStack() as ctx:
         keep = ctx.enter_context(tc.tile_pool(name="keep", bufs=1))
+        shared = ctx.enter_context(tc.tile_pool(name="shared", bufs=1))
         psum = ctx.enter_context(tc.psum_pool(name="psum", bufs=1))
 
         offsets = keep.tile([P, S // 16], U16, name="offsets")
@@ -36,28 +38,27 @@ def tile_picked_expool_exp_p_kernel(tc, x_words, x_scales, wa, wb, gt, gi, offs,
         x_plane = keep.tile([P, S], U8, name="x_plane", align_bytes=64)
         nc.vector.memset(x_plane[:].bitcast(I32), 0)
 
+        gi_sb = keep.tile([P, PACK], F32, name="gi_sb", align_bytes=64)
+        nc.sync.dma_start(gi_sb[:], gi.rearrange("(p t) o -> p (t o)", t=PACK))
+        gt_sb = keep.tile([P, PACK], F32, name="gt_sb", align_bytes=64)
+        nc.sync.dma_start(gt_sb[:], gt.rearrange("(p t) o -> p (t o)", t=PACK))
+
         word_table = keep.tile([P, T], I32, name="word_table", align_bytes=64)
         nc.sync.dma_start(word_table[:], x_words[0].rearrange("p c r -> p (c r)").bitcast(I32))
 
-        def load_half(w, half, name):
-            raw = keep.tile([P, PACK, HALF], F32, name=name, align_bytes=64)
+        def load_half(w, half, name, tag):
+            raw = keep.tile([P, PACK, HALF], F32, name=name, tag=tag, align_bytes=64)
             nc.sync.dma_start(raw[:], w.rearrange("(p j) c -> p j c", j=PACK)[:, :, half * HALF : (half + 1) * HALF])
             return raw
 
-        wb_raw = [load_half(wb, u, "wb_raw%d" % u) for u in range(2)]
-        wa_raw = [load_half(wa, u, "wa_raw%d" % u) for u in range(2)]
-
-        gi_sb = keep.tile([P, PACK], F32, name="gi_sb", align_bytes=64)
-        nc.gpsimd.dma_start(gi_sb[:], gi.rearrange("(p t) o -> p (t o)", t=PACK))
-        gt_sb = keep.tile([P, PACK], F32, name="gt_sb", align_bytes=64)
-        nc.gpsimd.dma_start(gt_sb[:], gt.rearrange("(p t) o -> p (t o)", t=PACK))
+        wb_raw = [load_half(wb, u, "wb_raw%d" % u, "wb_raw%d" % u) for u in range(2)]
 
         warm_in = keep.tile([P, 1], F32, name="warm_in")
         warm_out = keep.tile([P, 1], F32, name="warm_out")
         nc.gpsimd.memset(warm_in[:], 0.0)
         nc.scalar.activation(warm_out[:], warm_in[:], ACT.Exp, scale=0.5)
 
-        picked_scales = keep.tile([P, S], U8, name="picked_scales", align_bytes=64)
+        picked_scales = shared.tile([P, S], U8, name="picked_scales", align_bytes=64, offset=RAW_BYTES - S // 2)
         nc.vector.tensor_copy(picked_scales[:], scale_table[:].indirect(offsets[:]))
         dealt_scales = keep.tile([P, S], U8, name="dealt_scales", align_bytes=64)
         nc.vector.tensor_copy(
@@ -65,10 +66,16 @@ def tile_picked_expool_exp_p_kernel(tc, x_words, x_scales, wa, wb, gt, gi, offs,
             picked_scales[:].rearrange("p (c i t) -> p c t i", t=PACK, i=16),
         )
         for q in range(4):
-            nc.scalar.dma_start(
+            nc.sync.dma_start(
                 x_plane[32 * q : 32 * q + 4, :].bitcast(I32),
                 dealt_scales[32 * q : 32 * q + 32 : 8, :].bitcast(I32),
             )
+
+        wa_raw = [
+            shared.tile([P, PACK, HALF], F32, name="wa_raw%d" % u, align_bytes=64, offset=u * RAW_BYTES) for u in range(2)
+        ]
+        for u in range(2):
+            nc.sync.dma_start(wa_raw[u][:], wa.rearrange("(p j) c -> p j c", j=PACK)[:, :, u * HALF : (u + 1) * HALF])
 
         picked_words = keep.tile([P, S], I32, name="picked_words", tag="picked_then_codes", align_bytes=64)
         nc.vector.tensor_copy(picked_words[:].bitcast(U32), word_table[:].bitcast(U32).indirect(offsets[:]))
@@ -78,47 +85,60 @@ def tile_picked_expool_exp_p_kernel(tc, x_words, x_scales, wa, wb, gt, gi, offs,
             picked_words[:].rearrange("p (c i t) -> p c t i", t=PACK, i=4),
         )
 
-        def tiles(name, count, width, dtype):
-            return [keep.tile([P, width], dtype, name="%s%d" % (name, n), align_bytes=64) for n in range(count)]
+        def tile(name, width, dtype, tag):
+            return keep.tile([P, width], dtype, name=name, tag=tag, align_bytes=64)
 
-        wb_bf = tiles("wb_bf", 2, PACK * HALF, BF16)
-        wa_bf = tiles("wa_bf", 2, PACK * HALF, BF16)
-        wb_codes = [
-            keep.tile([P, HALF], I32, name="wb_codes0", tag="picked_then_codes", align_bytes=64),
-            keep.tile([P, HALF], I32, name="wb_codes1", align_bytes=64),
-        ]
-        wb_plane = tiles("wb_plane", 2, HALF, U8)
-        wa_codes, wa_plane = tiles("wa_codes", 2, HALF, I32), tiles("wa_plane", 2, HALF, U8)
-        z2_bf = tiles("z2_bf", 2, PACK * HALF, BF16)
-        z_bf = tiles("z_bf", 4, PACK * COLS, BF16)
-        e_sb = tiles("e_sb", 4, PACK * COLS, F32)
+        def tiles(name, count, width, dtype):
+            return [tile("%s%d" % (name, n), width, dtype, "%s%d" % (name, n)) for n in range(count)]
+
+        groups = [[0], [1], [2], [3, 4], [5], [6, 7]]
+        w_bf, w_codes, w_plane, group_bf = {}, {}, {}, []
+        group_codes, group_plane = [], []
+        first_codes = tile("first_codes", HALF, I32, "picked_then_codes")
+        for g, members in enumerate(groups):
+            bf = tile("w_bf%d" % g, PACK * COLS * len(members), BF16, "w_bf%d" % g)[:]
+            if g < 2:
+                codes = first_codes[:, g * COLS : (g + 1) * COLS]
+            else:
+                codes = tile("w_codes%d" % g, COLS * len(members), I32, "w_codes%d" % g)[:]
+            plane = tile("w_plane%d" % g, COLS * len(members), U8, "w_plane%d" % g)[:]
+            group_bf.append(bf)
+            group_codes.append(codes)
+            group_plane.append(plane)
+            for v, n in enumerate(members):
+                w_bf[n] = bf[:, v * PACK * COLS : (v + 1) * PACK * COLS]
+                w_codes[n] = codes[:, v * COLS : (v + 1) * COLS]
+                w_plane[n] = plane[:, v * COLS : (v + 1) * COLS]
+        w_raw = wb_raw + wa_raw
+        z2_pair = tiles("z2_pair", 2, PACK * HALF, BF16)
+        z_bf = [tile("z_bf%d" % n, PACK * COLS, BF16, "w_bf5" if n == 0 else "z_bf%d" % n) for n in range(4)]
+        e_sb = tiles("e_sb", 3, PACK * COLS, F32)
+        e_sb = [shared.tile([P, PACK * COLS], F32, name="e_first", align_bytes=64, offset=RAW_BYTES)] + e_sb
         z2_codes = keep.tile([P, N], I32, name="z2_codes", align_bytes=64)
         z2_plane = keep.tile([P, N], U8, name="z2_plane", align_bytes=64)
         z_codes, z_plane = tiles("z_codes", 4, COLS, I32), tiles("z_plane", 4, COLS, U8)
         result = tiles("result", 4, N, F32)
 
-        def cast(copy, raw, bf, n):
+        def cast(n):
             u, v = divmod(n, 2)
-            copy(
-                bf[u][:, v * PACK * COLS : (v + 1) * PACK * COLS].rearrange("p (c i j) -> p c j i", i=4, j=PACK),
-                raw[u][:, :, v * COLS : (v + 1) * COLS].rearrange("p j (c i) -> p c j i", i=4),
+            nc.scalar.copy(
+                w_bf[n].rearrange("p (c i j) -> p c j i", i=4, j=PACK),
+                w_raw[u][:, :, v * COLS : (v + 1) * COLS].rearrange("p j (c i) -> p c j i", i=4),
             )
 
         def quantize(codes, plane, values):
             nc.vector.quantize_mx(out=codes.bitcast(FP8X4), scales=plane, in_=values)
 
-        def project(codes, plane, n, bank):
-            u, v = divmod(n, 2)
-            acc = psum.tile([P, PACK, COLS], F32, name="acc", tag="bank%d" % bank)
-            cols = slice(v * COLS, (v + 1) * COLS)
+        def project(n):
+            acc = psum.tile([P, PACK, COLS], F32, name="acc", tag="bank%d" % n)
             for t in range(PACK):
                 places = slice(t * P, (t + 1) * P)
                 nc.tensor.matmul_mx(
                     out=acc[:, t, :],
                     lhsT=x_codes[:, places].bitcast(FP8X4),
                     lhsT_scale=x_plane[:, places],
-                    rhs=codes[u][:, cols].bitcast(FP8X4),
-                    rhs_scale=plane[u][:, cols],
+                    rhs=w_codes[n].bitcast(FP8X4),
+                    rhs_scale=w_plane[n],
                     start=True,
                     stop=True,
                 )
@@ -131,15 +151,18 @@ def tile_picked_expool_exp_p_kernel(tc, x_words, x_scales, wa, wb, gt, gi, offs,
 
         def values(n):
             u, v = divmod(n, 2)
-            weigh(z2_bf[u][:, v * PACK * COLS : (v + 1) * PACK * COLS], project(wb_codes, wb_plane, n, n), gi_sb)
+            weigh(z2_pair[u][:, v * PACK * COLS : (v + 1) * PACK * COLS], project(n), gi_sb)
 
         def quantize_values(u):
             cols = slice(u * HALF, (u + 1) * HALF)
-            quantize(z2_codes[:, cols], z2_plane[:, cols], z2_bf[u][:])
+            quantize(z2_codes[:, cols], z2_plane[:, cols], z2_pair[u][:])
+
+        def quantize_group(g):
+            quantize(group_codes[g], group_plane[g], group_bf[g])
 
         def scores(n):
             e = e_sb[n][:].rearrange("p (c t) -> p c t", t=PACK)
-            nc.scalar.activation(e, project(wa_codes, wa_plane, n, 4 + n), ACT.Exp, scale=0.5)
+            nc.scalar.activation(e, project(4 + n), ACT.Exp, scale=0.5)
 
         def weights(n):
             weigh(z_bf[n][:], e_sb[n][:].rearrange("p (c t) -> p c t", t=PACK), gt_sb)
@@ -171,25 +194,23 @@ def tile_picked_expool_exp_p_kernel(tc, x_words, x_scales, wa, wb, gt, gi, offs,
             pool_part(n, slice(0, N), n, False)
             store(n)
 
-        for v in range(2):
-            cast(nc.scalar.copy, wb_raw, wb_bf, v)
-            cols = slice(v * COLS, (v + 1) * COLS)
-            quantize(wb_codes[0][:, cols], wb_plane[0][:, cols], wb_bf[0][:, v * PACK * COLS : (v + 1) * PACK * COLS])
-        cast(nc.scalar.copy, wb_raw, wb_bf, 2)
-        cast(nc.scalar.copy, wb_raw, wb_bf, 3)
+        for n in range(3):
+            cast(n)
+            quantize_group(n)
+        cast(3)
         values(0)
         values(1)
-        quantize(wb_codes[1][:], wb_plane[1][:], wb_bf[1][:])
-        cast(nc.scalar.copy, wa_raw, wa_bf, 0)
-        cast(nc.scalar.copy, wa_raw, wa_bf, 1)
-        quantize_values(0)
+        cast(4)
         values(2)
-        quantize(wa_codes[0][:], wa_plane[0][:], wa_bf[0][:])
+        quantize_group(3)
+        cast(5)
+        quantize_values(0)
+        quantize_group(4)
         values(3)
-        cast(nc.scalar.copy, wa_raw, wa_bf, 2)
-        cast(nc.scalar.copy, wa_raw, wa_bf, 3)
+        cast(6)
+        cast(7)
+        quantize_group(5)
         quantize_values(1)
-        quantize(wa_codes[1][:], wa_plane[1][:], wa_bf[1][:])
         scores(0)
         scores(1)
         weights(0)
@@ -204,4 +225,5 @@ def tile_picked_expool_exp_p_kernel(tc, x_words, x_scales, wa, wb, gt, gi, offs,
         quantize_weights(3)
         pool_part(3, slice(0, HALF), 3, False)
         pool_part(3, slice(HALF, N), 4, True)
-        store(3)
+        nc.scalar.dma_start(out[3 * P : 4 * P, 0:HALF], result[3][:, 0:HALF])
+        nc.sync.dma_start(out[3 * P : 4 * P, HALF:N], result[3][:, HALF:N])

@@ -33,25 +33,24 @@ def tile_picked_expool_exp_p_kernel(tc, x_words, x_scales, wa, wb, gt, gi, offs,
         nc.sync.dma_start(offsets[:], offs)
 
         scale_table = keep.tile([P, T], U8, name="scale_table", align_bytes=64)
-        nc.vector.memset(scale_table[:].bitcast(I32), 0)
+        nc.vector.memset(scale_table[:, 0 : T // 2].bitcast(I32), 0)
+        nc.gpsimd.memset(scale_table[:, T // 2 : T].bitcast(I32), 0)
         nc.sync.dma_start(scale_table[0:P:8, :].bitcast(I32), x_scales[0].bitcast(I32))
         x_plane = keep.tile([P, S], U8, name="x_plane", align_bytes=64)
         nc.vector.memset(x_plane[:].bitcast(I32), 0)
 
         gi_sb = keep.tile([P, PACK], F32, name="gi_sb", align_bytes=64)
         nc.sync.dma_start(gi_sb[:], gi.rearrange("(p t) o -> p (t o)", t=PACK))
-        gt_sb = keep.tile([P, PACK], F32, name="gt_sb", align_bytes=64)
-        nc.sync.dma_start(gt_sb[:], gt.rearrange("(p t) o -> p (t o)", t=PACK))
 
         word_table = keep.tile([P, T], I32, name="word_table", align_bytes=64)
         nc.sync.dma_start(word_table[:], x_words[0].rearrange("p c r -> p (c r)").bitcast(I32))
 
-        def load_half(w, half, name, tag):
-            raw = keep.tile([P, PACK, HALF], F32, name=name, tag=tag, align_bytes=64)
-            nc.sync.dma_start(raw[:], w.rearrange("(p j) c -> p j c", j=PACK)[:, :, half * HALF : (half + 1) * HALF])
-            return raw
+        wb_all = keep.tile([P, PACK, N], F32, name="wb_all", align_bytes=64)
+        nc.sync.dma_start(wb_all[:], wb.rearrange("(p j) c -> p j c", j=PACK))
+        wb_raw = [wb_all[:, :, 0:HALF], wb_all[:, :, HALF:N]]
 
-        wb_raw = [load_half(wb, u, "wb_raw%d" % u, "wb_raw%d" % u) for u in range(2)]
+        gt_sb = keep.tile([P, PACK], F32, name="gt_sb", align_bytes=64)
+        nc.sync.dma_start(gt_sb[:], gt.rearrange("(p t) o -> p (t o)", t=PACK))
 
         warm_in = keep.tile([P, 1], F32, name="warm_in")
         warm_out = keep.tile([P, 1], F32, name="warm_out")
@@ -77,7 +76,7 @@ def tile_picked_expool_exp_p_kernel(tc, x_words, x_scales, wa, wb, gt, gi, offs,
         for u in range(2):
             nc.sync.dma_start(wa_raw[u][:], wa.rearrange("(p j) c -> p j c", j=PACK)[:, :, u * HALF : (u + 1) * HALF])
 
-        picked_words = keep.tile([P, S], I32, name="picked_words", tag="picked_then_codes", align_bytes=64)
+        picked_words = shared.tile([P, S], I32, name="picked_words", align_bytes=64, offset=16384)
         nc.vector.tensor_copy(picked_words[:].bitcast(U32), word_table[:].bitcast(U32).indirect(offsets[:]))
         x_codes = keep.tile([P, S], I32, name="x_codes", align_bytes=64)
         nc.vector.tensor_copy(
@@ -91,12 +90,17 @@ def tile_picked_expool_exp_p_kernel(tc, x_words, x_scales, wa, wb, gt, gi, offs,
         def tiles(name, count, width, dtype):
             return [tile("%s%d" % (name, n), width, dtype, "%s%d" % (name, n)) for n in range(count)]
 
-        groups = [[0], [1], [2], [3, 4], [5], [6, 7]]
+        groups = [[0], [1], [2], [3], [4, 5], [6, 7]]
         w_bf, w_codes, w_plane, group_bf = {}, {}, {}, []
         group_codes, group_plane = [], []
-        first_codes = tile("first_codes", HALF, I32, "picked_then_codes")
+        first_codes = shared.tile([P, HALF], I32, name="first_codes", align_bytes=64, offset=16384)
         for g, members in enumerate(groups):
-            bf = tile("w_bf%d" % g, PACK * COLS * len(members), BF16, "w_bf%d" % g)[:]
+            if g >= 4:
+                bf = shared.tile([P, PACK * HALF], BF16, name="w_bf%d" % g, align_bytes=64, offset=8192 + 1024 + (g - 4) * 4096)[:]
+            elif g == 0:
+                bf = shared.tile([P, PACK * COLS], BF16, name="w_bf0", align_bytes=64, offset=16384 + 1024)[:]
+            else:
+                bf = tile("w_bf%d" % g, PACK * COLS * len(members), BF16, "w_bf%d" % (1 if g == 3 else g))[:]
             if g < 2:
                 codes = first_codes[:, g * COLS : (g + 1) * COLS]
             else:
@@ -110,24 +114,37 @@ def tile_picked_expool_exp_p_kernel(tc, x_words, x_scales, wa, wb, gt, gi, offs,
                 w_codes[n] = codes[:, v * COLS : (v + 1) * COLS]
                 w_plane[n] = plane[:, v * COLS : (v + 1) * COLS]
         w_raw = wb_raw + wa_raw
-        z2_pair = tiles("z2_pair", 2, PACK * HALF, BF16)
-        z_bf = [tile("z_bf%d" % n, PACK * COLS, BF16, "w_bf5" if n == 0 else "z_bf%d" % n) for n in range(4)]
-        e_sb = tiles("e_sb", 3, PACK * COLS, F32)
-        e_sb = [shared.tile([P, PACK * COLS], F32, name="e_first", align_bytes=64, offset=RAW_BYTES)] + e_sb
-        z2_codes = keep.tile([P, N], I32, name="z2_codes", align_bytes=64)
+        z2_pair = tile("z2_pair", PACK * HALF, BF16, "z2_pair")
+        z2_bf = [
+            z2_pair[:, 0 : PACK * COLS],
+            z2_pair[:, PACK * COLS : PACK * HALF],
+            tile("z2_bf2", PACK * COLS, BF16, "z2_bf2")[:],
+            shared.tile([P, PACK * COLS], BF16, name="z2_bf3", align_bytes=64, offset=8192 + 1024)[:],
+        ]
+        z_bf = [
+            shared.tile([P, PACK * COLS], BF16, name="z_first%d" % n, align_bytes=64, offset=8192 + 1024 + 4096 + n * 1024)
+            for n in range(2)
+        ] + tiles("z_bf", 2, PACK * COLS, BF16)
+        e_sb = [
+            shared.tile([P, PACK * COLS], F32, name="e_first%d" % n, align_bytes=64, offset=RAW_BYTES + n * 2048)
+            for n in range(2)
+        ] + tiles("e_sb", 2, PACK * COLS, F32)
+        z2_codes = shared.tile([P, N], I32, name="z2_codes", align_bytes=64, offset=8192 + 2048)
         z2_plane = keep.tile([P, N], U8, name="z2_plane", align_bytes=64)
         z_codes, z_plane = tiles("z_codes", 4, COLS, I32), tiles("z_plane", 4, COLS, U8)
         result = tiles("result", 4, N, F32)
 
-        def cast(n):
-            u, v = divmod(n, 2)
-            nc.scalar.copy(
-                w_bf[n].rearrange("p (c i j) -> p c j i", i=4, j=PACK),
-                w_raw[u][:, :, v * COLS : (v + 1) * COLS].rearrange("p j (c i) -> p c j i", i=4),
+        def cast(g, copy):
+            u, v = divmod(groups[g][0], 2)
+            copy(
+                group_bf[g].rearrange("p (c i j) -> p c j i", i=4, j=PACK),
+                w_raw[u][:, :, v * COLS : (v + len(groups[g])) * COLS].rearrange("p j (c i) -> p c j i", i=4),
             )
 
         def quantize(codes, plane, values):
             nc.vector.quantize_mx(out=codes.bitcast(FP8X4), scales=plane, in_=values)
+
+        projected = {}
 
         def project(n):
             acc = psum.tile([P, PACK, COLS], F32, name="acc", tag="bank%d" % n)
@@ -142,30 +159,32 @@ def tile_picked_expool_exp_p_kernel(tc, x_words, x_scales, wa, wb, gt, gi, offs,
                     start=True,
                     stop=True,
                 )
-            return acc[:].rearrange("p t c -> p c t")
+            projected[n] = acc[:].rearrange("p t (c i) -> p c t i", i=2)
 
         def weigh(dst, src, g):
             nc.vector.tensor_tensor(
-                dst.rearrange("p (c t) -> p c t", t=PACK), src, g[:].unsqueeze(1).to_broadcast([P, COLS, PACK]), MULT
+                dst.rearrange("p (c i t) -> p c t i", t=PACK, i=2),
+                src,
+                g[:].unsqueeze(1).unsqueeze(3).to_broadcast([P, COLS // 2, PACK, 2]),
+                MULT,
             )
 
         def values(n):
-            u, v = divmod(n, 2)
-            weigh(z2_pair[u][:, v * PACK * COLS : (v + 1) * PACK * COLS], project(n), gi_sb)
+            weigh(z2_bf[n], projected[n], gi_sb)
 
-        def quantize_values(u):
-            cols = slice(u * HALF, (u + 1) * HALF)
-            quantize(z2_codes[:, cols], z2_plane[:, cols], z2_pair[u][:])
+        def quantize_values(first, count, src):
+            cols = slice(first * COLS, (first + count) * COLS)
+            quantize(z2_codes[:, cols], z2_plane[:, cols], src)
 
         def quantize_group(g):
             quantize(group_codes[g], group_plane[g], group_bf[g])
 
         def scores(n):
-            e = e_sb[n][:].rearrange("p (c t) -> p c t", t=PACK)
-            nc.scalar.activation(e, project(4 + n), ACT.Exp, scale=0.5)
+            e = e_sb[n][:].rearrange("p (c t i) -> p c t i", t=PACK, i=2)
+            nc.scalar.activation(e, projected[4 + n], ACT.Exp, scale=0.5)
 
         def weights(n):
-            weigh(z_bf[n][:], e_sb[n][:].rearrange("p (c t) -> p c t", t=PACK), gt_sb)
+            weigh(z_bf[n][:], e_sb[n][:].rearrange("p (c t i) -> p c t i", t=PACK, i=2), gt_sb)
 
         def quantize_weights(n):
             quantize(z_codes[n][:], z_plane[n][:], z_bf[n][:])
@@ -194,23 +213,25 @@ def tile_picked_expool_exp_p_kernel(tc, x_words, x_scales, wa, wb, gt, gi, offs,
             pool_part(n, slice(0, N), n, False)
             store(n)
 
-        for n in range(3):
-            cast(n)
-            quantize_group(n)
-        cast(3)
+        def prepare(g, copy):
+            cast(g, copy)
+            quantize_group(g)
+            for n in groups[g]:
+                project(n)
+
+        prepare(0, nc.vector.tensor_copy)
+        prepare(1, nc.scalar.copy)
+        prepare(2, nc.scalar.copy)
+        prepare(3, nc.vector.tensor_copy)
         values(0)
         values(1)
-        cast(4)
         values(2)
-        quantize_group(3)
-        cast(5)
-        quantize_values(0)
-        quantize_group(4)
+        prepare(4, nc.scalar.copy)
+        quantize_values(0, 2, z2_pair[:])
         values(3)
-        cast(6)
-        cast(7)
-        quantize_group(5)
-        quantize_values(1)
+        prepare(5, nc.scalar.copy)
+        quantize_values(2, 1, z2_bf[2])
+        quantize_values(3, 1, z2_bf[3])
         scores(0)
         scores(1)
         weights(0)
@@ -220,10 +241,10 @@ def tile_picked_expool_exp_p_kernel(tc, x_words, x_scales, wa, wb, gt, gi, offs,
         pool_out(0)
         weights(2)
         pool_out(1)
-        pool_out(2)
         weights(3)
-        quantize_weights(3)
-        pool_part(3, slice(0, HALF), 3, False)
-        pool_part(3, slice(HALF, N), 4, True)
-        nc.scalar.dma_start(out[3 * P : 4 * P, 0:HALF], result[3][:, 0:HALF])
-        nc.sync.dma_start(out[3 * P : 4 * P, HALF:N], result[3][:, HALF:N])
+        for n in (2, 3):
+            quantize_weights(n)
+        for n in (2, 3):
+            pool_part(n, slice(0, HALF), n, False)
+            pool_part(n, slice(HALF, N), n + 2, True)
+            store(n)

from contextlib import ExitStack

import concourse.mybir as mybir

K, T, S, H, N = 512, 2048, 512, 512, 512
FLOPS = 2 * K * S * H + 2 * K * S * N + 2 * S * H * N

F32 = mybir.dt.float32
BF16 = mybir.dt.bfloat16
I32 = mybir.dt.int32
U32 = mybir.dt.uint32
U16 = mybir.dt.uint16
U8 = mybir.dt.uint8
FP8X4 = mybir.dt.float8_e4m3fn_x4
ACT = mybir.ActivationFunctionType
MULT = mybir.AluOpType.mult

P = 128
PACK = 4
COLS = 128
HALF = 256
RAW_BYTES = PACK * HALF * 4


def tile_picked_expool_exp_p_kernel(tc, x_words, x_scales, wa, wb, gt, gi, offs, out):
    nc = tc.nc
    with ExitStack() as ctx:
        keep = ctx.enter_context(tc.tile_pool(name="keep", bufs=1))
        shared = ctx.enter_context(tc.tile_pool(name="shared", bufs=1))
        psum = ctx.enter_context(tc.psum_pool(name="psum", bufs=1))

        offsets = keep.tile([P, S // 16], U16, name="offsets")
        nc.sync.dma_start(offsets[:], offs)

        scale_table = keep.tile([P, T], U8, name="scale_table", align_bytes=64)
        nc.vector.memset(scale_table[:, 0 : T // 2].bitcast(I32), 0)
        nc.gpsimd.memset(scale_table[:, T // 2 : T].bitcast(I32), 0)
        nc.sync.dma_start(scale_table[0:P:8, :].bitcast(I32), x_scales[0].bitcast(I32))
        x_plane = keep.tile([P, S], U8, name="x_plane", align_bytes=64)
        nc.vector.memset(x_plane[:].bitcast(I32), 0)

        gi_sb = keep.tile([P, PACK], F32, name="gi_sb", align_bytes=64)
        nc.sync.dma_start(gi_sb[:], gi.rearrange("(p t) o -> p (t o)", t=PACK))

        word_table = keep.tile([P, T], I32, name="word_table", align_bytes=64)
        nc.sync.dma_start(word_table[:], x_words[0].rearrange("p c r -> p (c r)").bitcast(I32))

        wb_all = keep.tile([P, PACK, N], F32, name="wb_all", align_bytes=64)
        nc.sync.dma_start(wb_all[:], wb.rearrange("(p j) c -> p j c", j=PACK))
        wb_raw = [wb_all[:, :, 0:HALF], wb_all[:, :, HALF:N]]

        gt_sb = keep.tile([P, PACK], F32, name="gt_sb", align_bytes=64)
        nc.sync.dma_start(gt_sb[:], gt.rearrange("(p t) o -> p (t o)", t=PACK))

        warm_in = keep.tile([P, 1], F32, name="warm_in")
        warm_out = keep.tile([P, 1], F32, name="warm_out")
        nc.gpsimd.memset(warm_in[:], 0.0)
        nc.scalar.activation(warm_out[:], warm_in[:], ACT.Exp, scale=0.5)

        picked_scales = shared.tile([P, S], U8, name="picked_scales", align_bytes=64, offset=RAW_BYTES - S // 2)
        nc.vector.tensor_copy(picked_scales[:], scale_table[:].indirect(offsets[:]))
        dealt_scales = keep.tile([P, S], U8, name="dealt_scales", align_bytes=64)
        nc.vector.tensor_copy(
            dealt_scales[:].rearrange("p (t c i) -> p c t i", t=PACK, i=16),
            picked_scales[:].rearrange("p (c i t) -> p c t i", t=PACK, i=16),
        )
        for q in range(4):
            nc.sync.dma_start(
                x_plane[32 * q : 32 * q + 4, :].bitcast(I32),
                dealt_scales[32 * q : 32 * q + 32 : 8, :].bitcast(I32),
            )

        wa_raw = [
            shared.tile([P, PACK, HALF], F32, name="wa_raw%d" % u, align_bytes=64, offset=u * RAW_BYTES) for u in range(2)
        ]
        for u in range(2):
            nc.sync.dma_start(wa_raw[u][:], wa.rearrange("(p j) c -> p j c", j=PACK)[:, :, u * HALF : (u + 1) * HALF])

        picked_words = shared.tile([P, S], I32, name="picked_words", align_bytes=64, offset=16384)
        nc.vector.tensor_copy(picked_words[:].bitcast(U32), word_table[:].bitcast(U32).indirect(offsets[:]))
        x_codes = keep.tile([P, S], I32, name="x_codes", align_bytes=64)
        nc.vector.tensor_copy(
            x_codes[:].rearrange("p (t c i) -> p c t i", t=PACK, i=4),
            picked_words[:].rearrange("p (c i t) -> p c t i", t=PACK, i=4),
        )

        def tile(name, width, dtype, tag):
            return keep.tile([P, width], dtype, name=name, tag=tag, align_bytes=64)

        def tiles(name, count, width, dtype):
            return [tile("%s%d" % (name, n), width, dtype, "%s%d" % (name, n)) for n in range(count)]

        groups = [[0], [1], [2], [3], [4, 5], [6, 7]]
        w_bf, w_codes, w_plane, group_bf = {}, {}, {}, []
        group_codes, group_plane = [], []
        first_codes = shared.tile([P, HALF], I32, name="first_codes", align_bytes=64, offset=16384)
        for g, members in enumerate(groups):
            if g >= 4:
                bf = shared.tile([P, PACK * HALF], BF16, name="w_bf%d" % g, align_bytes=64, offset=8192 + 1024 + (g - 4) * 4096)[:]
            elif g == 0:
                bf = shared.tile([P, PACK * COLS], BF16, name="w_bf0", align_bytes=64, offset=16384 + 1024)[:]
            else:
                bf = tile("w_bf%d" % g, PACK * COLS * len(members), BF16, "w_bf%d" % (1 if g == 3 else g))[:]
            if g < 2:
                codes = first_codes[:, g * COLS : (g + 1) * COLS]
            else:
                codes = tile("w_codes%d" % g, COLS * len(members), I32, "w_codes%d" % g)[:]
            plane = tile("w_plane%d" % g, COLS * len(members), U8, "w_plane%d" % g)[:]
            group_bf.append(bf)
            group_codes.append(codes)
            group_plane.append(plane)
            for v, n in enumerate(members):
                w_bf[n] = bf[:, v * PACK * COLS : (v + 1) * PACK * COLS]
                w_codes[n] = codes[:, v * COLS : (v + 1) * COLS]
                w_plane[n] = plane[:, v * COLS : (v + 1) * COLS]
        w_raw = wb_raw + wa_raw
        z2_pair = tile("z2_pair", PACK * HALF, BF16, "z2_pair")
        z2_bf = [
            z2_pair[:, 0 : PACK * COLS],
            z2_pair[:, PACK * COLS : PACK * HALF],
            tile("z2_bf2", PACK * COLS, BF16, "z2_bf2")[:],
            shared.tile([P, PACK * COLS], BF16, name="z2_bf3", align_bytes=64, offset=8192 + 1024)[:],
        ]
        z_bf = [
            shared.tile([P, PACK * COLS], BF16, name="z_first%d" % n, align_bytes=64, offset=8192 + 1024 + 4096 + n * 1024)
            for n in range(2)
        ] + tiles("z_bf", 2, PACK * COLS, BF16)
        e_sb = [
            shared.tile([P, PACK * COLS], F32, name="e_first%d" % n, align_bytes=64, offset=RAW_BYTES + n * 2048)
            for n in range(2)
        ] + tiles("e_sb", 2, PACK * COLS, F32)
        z2_codes = shared.tile([P, N], I32, name="z2_codes", align_bytes=64, offset=8192 + 2048)
        z2_plane = keep.tile([P, N], U8, name="z2_plane", align_bytes=64)
        z_codes, z_plane = tiles("z_codes", 4, COLS, I32), tiles("z_plane", 4, COLS, U8)
        result = tiles("result", 4, N, F32)

        def cast(g, copy):
            u, v = divmod(groups[g][0], 2)
            copy(
                group_bf[g].rearrange("p (c i j) -> p c j i", i=4, j=PACK),
                w_raw[u][:, :, v * COLS : (v + len(groups[g])) * COLS].rearrange("p j (c i) -> p c j i", i=4),
            )

        def quantize(codes, plane, values):
            nc.vector.quantize_mx(out=codes.bitcast(FP8X4), scales=plane, in_=values)

        projected = {}

        def project(n):
            acc = psum.tile([P, PACK, COLS], F32, name="acc", tag="bank%d" % n)
            for t in range(PACK):
                places = slice(t * P, (t + 1) * P)
                nc.tensor.matmul_mx(
                    out=acc[:, t, :],
                    lhsT=x_codes[:, places].bitcast(FP8X4),
                    lhsT_scale=x_plane[:, places],
                    rhs=w_codes[n].bitcast(FP8X4),
                    rhs_scale=w_plane[n],
                    start=True,
                    stop=True,
                )
            projected[n] = acc[:].rearrange("p t (c i) -> p c t i", i=2)

        def weigh(dst, src, g):
            nc.vector.tensor_tensor(
                dst.rearrange("p (c i t) -> p c t i", t=PACK, i=2),
                src,
                g[:].unsqueeze(1).unsqueeze(3).to_broadcast([P, COLS // 2, PACK, 2]),
                MULT,
            )

        def values(n):
            weigh(z2_bf[n], projected[n], gi_sb)

        def quantize_values(first, count, src):
            cols = slice(first * COLS, (first + count) * COLS)
            quantize(z2_codes[:, cols], z2_plane[:, cols], src)

        def quantize_group(g):
            quantize(group_codes[g], group_plane[g], group_bf[g])

        def scores(n):
            e = e_sb[n][:].rearrange("p (c t i) -> p c t i", t=PACK, i=2)
            nc.scalar.activation(e, projected[4 + n], ACT.Exp, scale=0.5)

        def weights(n):
            weigh(z_bf[n][:], e_sb[n][:].rearrange("p (c t i) -> p c t i", t=PACK, i=2), gt_sb)

        def quantize_weights(n):
            quantize(z_codes[n][:], z_plane[n][:], z_bf[n][:])

        def pool_part(n, cols, bank, on_vector):
            acc = psum.tile([P, cols.stop - cols.start], F32, name="acc", tag="bank%d" % bank)
            nc.tensor.matmul_mx(
                out=acc[:],
                lhsT=z_codes[n][:].bitcast(FP8X4),
                lhsT_scale=z_plane[n][:],
                rhs=z2_codes[:, cols].bitcast(FP8X4),
                rhs_scale=z2_plane[:, cols],
                start=True,
                stop=True,
            )
            if on_vector:
                nc.vector.tensor_scalar_mul(result[n][:, cols], acc[:], 0.03125)
            else:
                nc.scalar.activation(result[n][:, cols], acc[:], ACT.Copy, scale=0.03125)

        def store(n):
            nc.sync.dma_start(out[n * P : (n + 1) * P, :], result[n][:])

        def pool_out(n):
            quantize_weights(n)
            pool_part(n, slice(0, N), n, False)
            store(n)

        def prepare(g, copy):
            cast(g, copy)
            quantize_group(g)
            for n in groups[g]:
                project(n)

        prepare(0, nc.vector.tensor_copy)
        prepare(1, nc.scalar.copy)
        prepare(2, nc.scalar.copy)
        prepare(3, nc.vector.tensor_copy)
        values(0)
        values(1)
        values(2)
        prepare(4, nc.scalar.copy)
        quantize_values(0, 2, z2_pair[:])
        values(3)
        prepare(5, nc.scalar.copy)
        quantize_values(2, 1, z2_bf[2])
        quantize_values(3, 1, z2_bf[3])
        scores(0)
        scores(1)
        weights(0)
        scores(2)
        weights(1)
        scores(3)
        pool_out(0)
        weights(2)
        pool_out(1)
        weights(3)
        for n in (2, 3):
            quantize_weights(n)
        for n in (2, 3):
            pool_part(n, slice(0, HALF), n, False)
            pool_part(n, slice(HALF, N), n + 2, True)
            store(n)
